import numpy as np
import ml_dtypes


def mxq(x, axis, fmt="e4m3"):
    dtype, down = {"e4m3": (ml_dtypes.float8_e4m3fn, 7), "e5m2": (ml_dtypes.float8_e5m2, 14)}[fmt]
    v = np.moveaxis(np.asarray(x, np.float32).astype(ml_dtypes.bfloat16).astype(np.float64), axis, -1)
    blocks = v.reshape(v.shape[:-1] + (-1, 32))
    amax = np.abs(blocks).max(-1, keepdims=True)
    byte = np.maximum(np.where(amax > 0, np.frexp(amax)[1] - 1 + 127, 0) - down, 1)
    scale = np.exp2(byte - 127.0)
    codes = (blocks / scale).astype(np.float32).astype(dtype).astype(np.float64)
    return np.moveaxis((codes * scale).reshape(v.shape), -1, axis)


WIDE = False


def mx_kscale(k):
    if not WIDE:
        return np.ones(k)
    levels = np.array([10, -10, 5, -5, 0])
    if k % 512:
        return np.exp2(np.random.permutation(np.resize(levels, k // 32))).repeat(32)
    a = np.empty((k // 512, 16))
    for p in range(k // 512):
        a[p, :8] = np.random.permutation(np.resize(levels, 8))
        for g in range(8):
            far = levels[np.abs(levels - a[p, g]) >= 10]
            a[p, g + 8] = far[np.random.randint(len(far))]
    return np.exp2(a.ravel()).repeat(32)


BF16 = ml_dtypes.bfloat16


def bf(x):
    return np.asarray(x, np.float32).astype(BF16)


def f64(x):
    return np.asarray(x).astype(np.float64)


E2M1 = np.array([0.0, 0.5, 1.0, 1.5, 2.0, 3.0, 4.0, 6.0, -0.0, -0.5, -1.0, -1.5, -2.0, -3.0, -4.0, -6.0])


def pack_weight(w, fmt):
    k, n = w.shape
    w = f64(bf(w)).reshape(k // 32, 32, n)
    amax = np.abs(w).max(1)
    if fmt == "e4m3":
        byte = np.frexp(amax)[1] - 1 + 127 - 7
    else:
        mant, ex = np.frexp(amax / 6.0)
        byte = np.where(mant > 0.5, ex, ex - 1) + 127
    byte = np.clip(np.where(amax > 0, byte, 1), 1, 254)
    scaled = (w * np.exp2(127.0 - byte)[:, None, :]).reshape(k, n).astype(np.float32)
    by_word = np.ascontiguousarray(scaled.reshape(k // 512, 128, 4, n).transpose(0, 1, 3, 2))
    if fmt == "e4m3":
        words = by_word.astype(ml_dtypes.float8_e4m3fn).view(np.uint8)
    else:
        c = by_word.astype(ml_dtypes.float4_e2m1fn).view(np.uint8) & 0xF
        words = c[..., 0::2] | (c[..., 1::2] << 4)
    return np.ascontiguousarray(words), np.ascontiguousarray(byte.astype(np.uint8).reshape(k // 512, 16, n))


def unpack_weight(words, scales, fmt):
    g, p, n, _ = words.shape
    if fmt == "e4m3":
        vals = np.ascontiguousarray(words).view(ml_dtypes.float8_e4m3fn).astype(np.float64)
    else:
        nib = np.empty((g, p, n, 4), np.uint8)
        nib[..., 0::2] = words & 0xF
        nib[..., 1::2] = words >> 4
        vals = E2M1[nib]
    vals = vals * np.repeat(np.exp2(scales.astype(np.float64) - 127.0), 8, axis=1)[..., None]
    return vals.transpose(0, 1, 3, 2).reshape(g * 512, n)
def pack4(w):
    words, scales = pack_weight(w, "e2m1")
    return words.reshape(words.shape[0], 128, -1), scales


def unpack4(words, scales):
    return unpack_weight(words.reshape(words.shape[0], 128, -1, 2), scales, "e2m1")


T, V, C, D, P = 2048, 512, 512, 1024, 1536


def setup_inputs():
    s, u, r = mx_kscale(V), mx_kscale(C), mx_kscale(D)
    scatter = np.random.standard_normal((T, V)) / np.sqrt(V)
    latents = np.random.standard_normal((V, D))
    feats = np.random.standard_normal((T, C))
    w_pos = np.random.standard_normal((C, D)) / np.sqrt(C)
    w_head = np.random.standard_normal((D, P)) / np.sqrt(D)
    pos_words, pos_scales = pack4(w_pos / u[:, None] * r)
    head_words, head_scales = pack4(w_head / r[:, None])
    mean = 0.5 * np.random.standard_normal(T)
    std = 0.5 + np.random.random(T)
    pixels = mean[:, None] + std[:, None] * np.random.standard_normal((T, P))
    return {"scatter": bf(scatter * s),
            "latents": bf(latents / s[:, None] * r),
            "feats": bf(feats * u),
            "pos_words": pos_words, "pos_scales": pos_scales,
            "masked": bf(np.random.permutation(T) >= V),
            "embed": bf(np.random.standard_normal(D) * r),
            "head_words": head_words, "head_scales": head_scales,
            "pixels": bf(pixels), "mean": bf(mean), "rstd": bf(1 / std)}


def reference(scatter, latents, feats, pos_words, pos_scales, masked, embed, head_words, head_scales, pixels, mean, rstd):
    spread = mxq(f64(scatter), 1, "e4m3") @ mxq(f64(latents), 0, "e4m3")
    placed = mxq(f64(feats), 1, "e4m3") @ unpack4(pos_words, pos_scales)
    full = spread + placed + f64(masked)[:, None] * f64(embed)
    pred = mxq(full, 1, "e4m3") @ unpack4(head_words, head_scales)
    target = (f64(pixels) - f64(mean)[:, None]) * f64(rstd)[:, None]
    return pred - target

@@ -1,0 +1,325 @@
+from contextlib import ExitStack
+
+import concourse.mybir as mybir
+from concourse.masks import make_identity
+
+T, V, C, D, PIX = 2048, 512, 512, 1024, 1536
+FLOPS = 2 * T * (V * D + C * D + D * PIX)
+
+F32 = mybir.dt.float32
+BF16 = mybir.dt.bfloat16
+I32 = mybir.dt.int32
+U32 = mybir.dt.uint32
+U8 = mybir.dt.uint8
+FP8X4 = mybir.dt.float8_e4m3fn_x4
+FP4X4 = mybir.dt.float4_e2m1fn_x4
+ALU = mybir.AluOpType
+ACT = mybir.ActivationFunctionType
+
+P = 128
+PACK = 4
+BANK = 512
+TILES = T // P
+CHUNK_TILES = BANK // P
+CHUNKS = TILES // CHUNK_TILES
+GROUPS = D // (P * PACK)
+PIX_BANKS = PIX // BANK
+
+
+def tile_patch_reconstruction_residual_s3_kernel(
+    tc, scatter, latents, feats, pos_words, pos_scales, masked, embed, head_words, head_scales, pixels, mean, rstd, out
+):
+    nc = tc.nc
+
+    with ExitStack() as ctx:
+        keep = ctx.enter_context(tc.tile_pool(name="keep", bufs=1))
+        flow = ctx.enter_context(tc.tile_pool(name="flow", bufs=1))
+        psum = ctx.enter_context(tc.psum_pool(name="psum", bufs=1))
+        ctx.enter_context(tc.manual_schedule())
+
+        by_tile = {
+            "s": scatter.rearrange("(p i) k -> p i k", i=TILES),
+            "f": feats.rearrange("(p i) k -> p i k", i=TILES),
+        }
+        pixels_v = pixels.rearrange("(p i) n -> p i n", i=TILES)
+        out_v = out.rearrange("(p i) n -> p i n", i=TILES)
+        latents_v = latents.rearrange("(p j) d -> p j d", j=PACK)
+
+        ident = keep.tile([P, P], F32, name="ident")
+        ident_bf = keep.tile([P, P], BF16, name="ident_bf")
+        pos_w_raw = keep.tile([P, 2 * D], U8, name="pos_w_raw", align_bytes=64)
+        pos_s_raw = keep.tile([P, D], U8, name="pos_s_raw", align_bytes=64)
+        pos_w = [keep.tile([P, D], U8, name="pos_w%d" % g, align_bytes=64) for g in range(GROUPS)]
+        pos_s = [keep.tile([P, D // 2], U8, name="pos_s%d" % g, align_bytes=64) for g in range(GROUPS)]
+        head_w = keep.tile([P, GROUPS, 2 * PIX], U8, name="head_w", align_bytes=64)
+        head_s = keep.tile([P, GROUPS, PIX], U8, name="head_s", align_bytes=64)
+        lat_raw = [keep.tile([P, PACK, BANK], BF16, name="lat_raw%d" % g) for g in range(GROUPS)]
+        lat_k4 = [keep.tile([P, BANK * PACK], BF16, name="lat_k4%d" % g, align_bytes=64) for g in range(GROUPS)]
+        lat_c = [keep.tile([P, BANK], U32, name="lat_c%d" % g, align_bytes=64) for g in range(GROUPS)]
+        lat_s = [keep.tile([P, BANK], U8, name="lat_s%d" % g, align_bytes=64) for g in range(GROUPS)]
+        mask_col = keep.tile([P, TILES], BF16, name="mask_col")
+        mean_col = keep.tile([P, TILES], BF16, name="mean_col")
+        rstd_col = keep.tile([P, TILES], BF16, name="rstd_col")
+        rstd_f32 = keep.tile([P, TILES], F32, name="rstd_f32")
+        shift = keep.tile([P, TILES], F32, name="shift")
+        embed_col = keep.tile([P, GROUPS, PACK], BF16, name="embed_col")
+        mask_row = keep.tile([P, T], BF16, name="mask_row")
+
+        x_raw, x_k4, x_q = {}, {}, {}
+        pix, target = {}, {}
+        planes, full_k4, full_q, acc1 = {}, {}, {}, {}
+
+        def load_x(name, c):
+            raw = keep.tile([P, CHUNK_TILES, V], BF16, name="raw_%s%d" % (name, c))
+            nc.sync.dma_start(out=raw[:], in_=by_tile[name][:, CHUNK_TILES * c : CHUNK_TILES * (c + 1), :])
+            x_raw[name, c] = raw
+
+        def load_pixels(c):
+            rows = flow.tile([P, CHUNK_TILES, PIX], BF16, name="pix", bufs=3)
+            nc.sync.dma_start(out=rows[:], in_=pixels_v[:, CHUNK_TILES * c : CHUNK_TILES * (c + 1), :])
+            pix[c] = rows
+
+        def load_latents(g):
+            nc.sync.dma_start(out=lat_raw[g][:], in_=latents_v[:, :, BANK * g : BANK * (g + 1)])
+
+        def turn_x(name, c):
+            words = x_raw[name, c][:].rearrange("p i k -> p (i k)").bitcast(F32)
+            k4 = flow.tile([P, BANK * PACK], BF16, name="x_k4", bufs=3, align_bytes=64)
+            k4_words = k4[:].bitcast(F32).rearrange("p (i r u) -> p i r u", i=CHUNK_TILES, u=2)
+            banks = []
+            for h in range(2):
+                bank = psum.tile([P, 2, 2, P], F32, name="turn", bufs=2)
+                for i in range(2):
+                    w0 = (V // 2) * (2 * h + i)
+                    for u in range(2):
+                        nc.tensor.transpose(bank[:, i, u, :], words[:, w0 + u : w0 + V // 2 : 2], ident[:])
+                banks.append(bank)
+            for h in range(2):
+                nc.scalar.copy(out=k4_words[:, 2 * h : 2 * h + 2, :, :], in_=banks[h][:].rearrange("p i u r -> p i r u"))
+            x_k4[name, c] = k4
+
+        def quantize(src, tag, bufs):
+            codes = flow.tile([P, BANK], U32, name=tag + "_c", bufs=bufs, align_bytes=64)
+            scales = flow.tile([P, BANK], U8, name=tag + "_s", bufs=bufs, align_bytes=64)
+            nc.vector.quantize_mx(out=codes[:].bitcast(FP8X4), scales=scales[:], in_=src[:])
+            return codes, scales
+
+        def quantize_x(name, c):
+            x_q[name, c] = quantize(x_k4[name, c], "xq", 4)
+
+        def quantize_full(c, g):
+            full_q[c, g] = quantize(full_k4[c, g], "fq", 4)
+
+        def sort_pos(g):
+            nc.vector.tensor_copy(
+                out=pos_w[g][:].rearrange("p (t m b) -> p t m b", t=PACK, b=2),
+                in_=pos_w_raw[:, D * g : D * (g + 1)].rearrange("p (m t b) -> p t m b", t=PACK, b=2),
+            )
+            nc.vector.tensor_copy(
+                out=pos_s[g][:].rearrange("p (t m) -> p t m", t=PACK),
+                in_=pos_s_raw[:, BANK * g : BANK * (g + 1)].rearrange("p (m t) -> p t m", t=PACK),
+            )
+
+        def sort_latents(g, copy):
+            copy(
+                out=lat_k4[g][:].rearrange("p (t m j) -> p t m j", t=PACK, j=PACK),
+                in_=lat_raw[g][:].rearrange("p j (m t) -> p t m j", t=PACK),
+            )
+
+        def quantize_latents(g):
+            nc.vector.quantize_mx(out=lat_c[g][:].bitcast(FP8X4), scales=lat_s[g][:], in_=lat_k4[g][:])
+
+        def open_full(c, g, t):
+            bank = psum.tile([P, BANK], F32, name="mx", bufs=6)
+            codes, scales = x_q["f", c]
+            nc.tensor.matmul_mx(
+                out=bank[:],
+                lhsT=pos_w[g][:, 2 * P * t : 2 * P * (t + 1)].bitcast(FP4X4),
+                lhsT_scale=pos_s[g][:, P * t : P * (t + 1)],
+                rhs=codes[:].bitcast(FP8X4),
+                rhs_scale=scales[:],
+                start=True,
+                stop=False,
+            )
+            acc1[c, g, t] = bank
+
+        def close_full(c, g, t):
+            bank = acc1[c, g, t]
+            codes, scales = x_q["s", c]
+            nc.tensor.matmul_mx(
+                out=bank[:],
+                lhsT=lat_c[g][:, P * t : P * (t + 1)].bitcast(FP8X4),
+                lhsT_scale=lat_s[g][:, P * t : P * (t + 1)],
+                rhs=codes[:].bitcast(FP8X4),
+                rhs_scale=scales[:],
+                start=False,
+                stop=True,
+            )
+            if t == 0:
+                planes[c, g] = flow.tile([P, PACK, BANK], BF16, name="planes", bufs=3)
+            nc.vector.scalar_tensor_tensor(
+                out=planes[c, g][:, t, :],
+                in0=mask_row[:, BANK * c : BANK * (c + 1)],
+                scalar=embed_col[:, g, t : t + 1],
+                in1=bank[:],
+                op0=ALU.mult,
+                op1=ALU.add,
+            )
+
+        def full_bank(c, b):
+            g, t = divmod(b, PACK)
+            open_full(c, g, t)
+            close_full(c, g, t)
+
+        def weave_full(c, g):
+            k4 = flow.tile([P, BANK * PACK], BF16, name="full_k4", bufs=3, align_bytes=64)
+            nc.scalar.copy(
+                out=k4[:].rearrange("p (q i t) -> p q t i", i=4, t=PACK),
+                in_=planes[c, g][:].rearrange("p t (q i) -> p q t i", i=4),
+            )
+            full_k4[c, g] = k4
+
+        def normalise(i, on_pool):
+            c, ii = divmod(i, CHUNK_TILES)
+            rows = flow.tile([P, PIX], F32, name="rows", bufs=8)
+            if on_pool:
+                for n in range(PIX_BANKS):
+                    cols = slice(BANK * n, BANK * (n + 1))
+                    nc.gpsimd.tensor_scalar(
+                        out=rows[:, cols],
+                        in0=pix[c][:, ii, cols],
+                        scalar1=rstd_f32[:, i : i + 1],
+                        scalar2=shift[:, i : i + 1],
+                        op0=ALU.mult,
+                        op1=ALU.add,
+                    )
+            else:
+                nc.scalar.activation(
+                    out=rows[:], in_=pix[c][:, ii, :], func=ACT.Identity, bias=shift[:, i : i + 1], scale=rstd_f32[:, i : i + 1]
+                )
+            target[i] = rows
+
+        def pred_bank(c, b):
+            ii, n = divmod(b, PIX_BANKS)
+            i = CHUNK_TILES * c + ii
+            cols = slice(BANK * n, BANK * (n + 1))
+            bank = psum.tile([P, BANK], F32, name="mx", bufs=6)
+            for g in range(GROUPS):
+                codes, scales = full_q[c, g]
+                nc.tensor.matmul_mx(
+                    out=bank[:],
+                    lhsT=codes[:, P * ii : P * (ii + 1)].bitcast(FP8X4),
+                    lhsT_scale=scales[:, P * ii : P * (ii + 1)],
+                    rhs=head_w[:, g, 2 * BANK * n : 2 * BANK * (n + 1)].bitcast(FP4X4),
+                    rhs_scale=head_s[:, g, cols],
+                    start=(g == 0),
+                    stop=(g == GROUPS - 1),
+                )
+            nc.vector.tensor_tensor(out=target[i][:, cols], in0=bank[:], in1=target[i][:, cols], op=ALU.subtract)
+            if i == TILES - 1:
+                nc.sync.dma_start(out=out_v[:, i, cols], in_=target[i][:, cols])
+            elif n == PIX_BANKS - 1:
+                nc.sync.dma_start(out=out_v[:, i, :], in_=target[i][:])
+
+        nc.vector.memset(pos_s_raw[:].bitcast(I32), 0)
+        nc.vector.memset(head_s[:].rearrange("p g n -> p (g n)").bitcast(I32), 0)
+        make_identity(nc, ident[:])
+        nc.scalar.activation(out=ident_bf[:], in_=ident[:], func=ACT.Identity)
+
+        nc.sync.dma_start(out=pos_w_raw[:].bitcast(I32), in_=pos_words[0].bitcast(I32))
+        for q in range(4):
+            nc.sync.dma_start(
+                out=pos_s_raw[32 * q : 32 * q + 4, :].bitcast(I32), in_=pos_scales[0, 4 * q : 4 * q + 4, :].bitcast(I32)
+            )
+        load_x("f", 0)
+        load_x("s", 0)
+        load_latents(0)
+        nc.sync.dma_start(out=mask_col[:], in_=masked.rearrange("(p i) -> p i", i=TILES))
+        nc.sync.dma_start(out=embed_col[:], in_=embed.rearrange("(g p t) -> p g t", g=GROUPS, t=PACK))
+        load_latents(1)
+        nc.sync.dma_start(out=mean_col[:], in_=mean.rearrange("(p i) -> p i", i=TILES))
+        nc.sync.dma_start(out=rstd_col[:], in_=rstd.rearrange("(p i) -> p i", i=TILES))
+        load_x("s", 1)
+        load_x("f", 1)
+        for q in range(4):
+            nc.sync.dma_start(
+                out=head_s[32 * q : 32 * q + 4, :, :].bitcast(I32),
+                in_=head_scales[:, 4 * q : 4 * q + 4, :].rearrange("g r n -> r g n").bitcast(I32),
+            )
+        nc.sync.dma_start(out=head_w[:].bitcast(I32), in_=head_words.rearrange("g p n -> p g n").bitcast(I32))
+        load_pixels(0)
+        load_x("s", 2)
+        load_x("f", 2)
+        load_pixels(1)
+        load_x("s", 3)
+        load_x("f", 3)
+
+        sort_pos(0)
+        sort_pos(1)
+        turn_x("f", 0)
+        turn_x("s", 0)
+        quantize_x("f", 0)
+        for t in range(PACK):
+            open_full(0, 0, t)
+        for h in range(2):
+            bank = psum.tile([P, TILES // 2, P], BF16, name="turn", bufs=2)
+            for i in range(TILES // 2):
+                col = TILES // 2 * h + i
+                nc.tensor.transpose(bank[:, i, :], mask_col[:, col : col + 1].to_broadcast([P, P]), ident_bf[:])
+            nc.scalar.copy(out=mask_row[:, T // 2 * h : T // 2 * (h + 1)], in_=bank[:].rearrange("p i m -> p (i m)"))
+        sort_latents(0, nc.vector.tensor_copy)
+        quantize_x("s", 0)
+        quantize_latents(0)
+        sort_latents(1, nc.scalar.copy)
+        nc.vector.tensor_copy(out=rstd_f32[:], in_=rstd_col[:])
+        nc.vector.scalar_tensor_tensor(
+            out=shift[:], in0=mean_col[:], scalar=-1.0, in1=rstd_col[:], op0=ALU.mult, op1=ALU.mult
+        )
+        for t in range(PACK):
+            close_full(0, 0, t)
+            if t == 1:
+                quantize_latents(1)
+        turn_x("s", 1)
+        full_bank(0, 4)
+        full_bank(0, 5)
+        turn_x("f", 1)
+        quantize_x("s", 1)
+        weave_full(0, 0)
+        full_bank(0, 6)
+        quantize_x("f", 1)
+        full_bank(0, 7)
+        weave_full(0, 1)
+        for i in range(CHUNK_TILES):
+            normalise(i, True)
+
+        for c in range(1, CHUNKS + 1):
+            more = c + 1 < CHUNKS
+            if c < CHUNKS:
+                quantize_at = (3, 6) if c == 1 else ((0, 2) if more else (-1, -1))
+                for b in range(GROUPS * PACK):
+                    full_bank(c, b)
+                    if b == 1 and more:
+                        turn_x("s", c + 1)
+                    if b == PACK - 1:
+                        weave_full(c, 0)
+                    if b in quantize_at:
+                        quantize_full(c - 1, quantize_at.index(b))
+                    if c == CHUNKS - 1 and b in (0, 2):
+                        quantize_full(c - 1, b // 2)
+                if more:
+                    turn_x("f", c + 1)
+                weave_full(c, 1)
+                for ii in range(CHUNK_TILES):
+                    normalise(CHUNK_TILES * c + ii, ii < 2)
+            for b in range(CHUNK_TILES * PIX_BANKS):
+                pred_bank(c - 1, b)
+                if more and b == 2:
+                    quantize_x("s", c + 1)
+                if more and b == 5:
+                    quantize_x("f", c + 1)
+                if c == CHUNKS - 1 and b == 2:
+                    quantize_full(c, 0)
+                if c == CHUNKS - 1 and b == 6:
+                    quantize_full(c, 1)
+                if more and b == 5:
+                    load_pixels(c + 1)

@@ -24,6 +24,10 @@ CHUNK_TILES = BANK // P
 CHUNKS = TILES // CHUNK_TILES
 GROUPS = D // (P * PACK)
 PIX_BANKS = PIX // BANK
+POOL_TILES = (0, 1, 2, 7, 11, 15)
+ORDER = [("full", b) for b in range(4)]
+ORDER = ORDER + [step for b in range(4) for step in (("pred", b), ("full", 4 + b))] + [("pred", b) for b in range(4, 12)]
+ORDER_FIRST = [("full", b) for b in range(8)] + [("pred", b) for b in range(12)]
 
 
 def tile_patch_reconstruction_residual_s3_kernel(
@@ -65,7 +69,7 @@ def tile_patch_reconstruction_residual_s3_kernel(
         embed_col = keep.tile([P, GROUPS, PACK], BF16, name="embed_col")
         mask_row = keep.tile([P, T], BF16, name="mask_row")
 
-        x_raw, x_k4, x_q = {}, {}, {}
+        x_raw, turned, x_k4, x_q = {}, {}, {}, {}
         pix, target = {}, {}
         planes, full_k4, full_q, acc1 = {}, {}, {}, {}
 
@@ -74,18 +78,24 @@ def tile_patch_reconstruction_residual_s3_kernel(
             nc.sync.dma_start(out=raw[:], in_=by_tile[name][:, CHUNK_TILES * c : CHUNK_TILES * (c + 1), :])
             x_raw[name, c] = raw
 
-        def load_pixels(c):
-            rows = flow.tile([P, CHUNK_TILES, PIX], BF16, name="pix", bufs=3)
-            nc.sync.dma_start(out=rows[:], in_=pixels_v[:, CHUNK_TILES * c : CHUNK_TILES * (c + 1), :])
-            pix[c] = rows
+        def load_pixels(i, count):
+            part = keep.tile([P, count, PIX], BF16, name="pix%d" % i)
+            nc.sync.dma_start(out=part[:], in_=pixels_v[:, i : i + count, :])
+            for k in range(count):
+                pix[i + k] = part[:, k, :]
+
+        def spread_mask(h):
+            bank = psum.tile([P, TILES // 2, P], BF16, name="mx", bufs=6)
+            for ii in range(TILES // 2):
+                i = TILES // 2 * h + ii
+                nc.tensor.transpose(bank[:, ii, :], mask_col[:, i : i + 1].to_broadcast([P, P]), ident_bf[:])
+            nc.scalar.copy(out=mask_row[:, T // 2 * h : T // 2 * (h + 1)], in_=bank[:].rearrange("p i m -> p (i m)"))
 
         def load_latents(g):
             nc.sync.dma_start(out=lat_raw[g][:], in_=latents_v[:, :, BANK * g : BANK * (g + 1)])
 
         def turn_x(name, c):
             words = x_raw[name, c][:].rearrange("p i k -> p (i k)").bitcast(F32)
-            k4 = flow.tile([P, BANK * PACK], BF16, name="x_k4", bufs=3, align_bytes=64)
-            k4_words = k4[:].bitcast(F32).rearrange("p (i r u) -> p i r u", i=CHUNK_TILES, u=2)
             banks = []
             for h in range(2):
                 bank = psum.tile([P, 2, 2, P], F32, name="turn", bufs=2)
@@ -94,8 +104,13 @@ def tile_patch_reconstruction_residual_s3_kernel(
                     for u in range(2):
                         nc.tensor.transpose(bank[:, i, u, :], words[:, w0 + u : w0 + V // 2 : 2], ident[:])
                 banks.append(bank)
-            for h in range(2):
-                nc.scalar.copy(out=k4_words[:, 2 * h : 2 * h + 2, :, :], in_=banks[h][:].rearrange("p i u r -> p i r u"))
+            turned[name, c] = banks
+
+        def empty_x(name, c):
+            k4 = flow.tile([P, BANK * PACK], BF16, name="x_k4", bufs=3, align_bytes=64)
+            k4_words = k4[:].bitcast(F32).rearrange("p (i r u) -> p i r u", i=CHUNK_TILES, u=2)
+            for h, bank in enumerate(turned[name, c]):
+                nc.scalar.copy(out=k4_words[:, 2 * h : 2 * h + 2, :, :], in_=bank[:].rearrange("p i u r -> p i r u"))
             x_k4[name, c] = k4
 
         def quantize(src, tag, bufs):
@@ -129,47 +144,41 @@ def tile_patch_reconstruction_residual_s3_kernel(
         def quantize_latents(g):
             nc.vector.quantize_mx(out=lat_c[g][:].bitcast(FP8X4), scales=lat_s[g][:], in_=lat_k4[g][:])
 
-        def open_full(c, g, t):
-            bank = psum.tile([P, BANK], F32, name="mx", bufs=6)
-            codes, scales = x_q["f", c]
+        def full_pass(name, c, g, t, start):
+            if start:
+                acc1[c, g, t] = psum.tile([P, BANK], F32, name="mx", bufs=6)
+            codes, scales = x_q[name, c]
+            if name == "s":
+                weights, weight_scales = lat_c[g][:, P * t : P * (t + 1)].bitcast(FP8X4), lat_s[g]
+            else:
+                weights, weight_scales = pos_w[g][:, 2 * P * t : 2 * P * (t + 1)].bitcast(FP4X4), pos_s[g]
             nc.tensor.matmul_mx(
-                out=bank[:],
-                lhsT=pos_w[g][:, 2 * P * t : 2 * P * (t + 1)].bitcast(FP4X4),
-                lhsT_scale=pos_s[g][:, P * t : P * (t + 1)],
+                out=acc1[c, g, t][:],
+                lhsT=weights,
+                lhsT_scale=weight_scales[:, P * t : P * (t + 1)],
                 rhs=codes[:].bitcast(FP8X4),
                 rhs_scale=scales[:],
-                start=True,
-                stop=False,
+                start=start,
+                stop=not start,
             )
-            acc1[c, g, t] = bank
 
-        def close_full(c, g, t):
-            bank = acc1[c, g, t]
-            codes, scales = x_q["s", c]
-            nc.tensor.matmul_mx(
-                out=bank[:],
-                lhsT=lat_c[g][:, P * t : P * (t + 1)].bitcast(FP8X4),
-                lhsT_scale=lat_s[g][:, P * t : P * (t + 1)],
-                rhs=codes[:].bitcast(FP8X4),
-                rhs_scale=scales[:],
-                start=False,
-                stop=True,
-            )
+        def empty_full(c, g, t):
             if t == 0:
                 planes[c, g] = flow.tile([P, PACK, BANK], BF16, name="planes", bufs=3)
             nc.vector.scalar_tensor_tensor(
                 out=planes[c, g][:, t, :],
                 in0=mask_row[:, BANK * c : BANK * (c + 1)],
                 scalar=embed_col[:, g, t : t + 1],
-                in1=bank[:],
+                in1=acc1[c, g, t][:],
                 op0=ALU.mult,
                 op1=ALU.add,
             )
 
         def full_bank(c, b):
             g, t = divmod(b, PACK)
-            open_full(c, g, t)
-            close_full(c, g, t)
+            full_pass("s", c, g, t, True)
+            full_pass("f", c, g, t, False)
+            empty_full(c, g, t)
 
         def weave_full(c, g):
             k4 = flow.tile([P, BANK * PACK], BF16, name="full_k4", bufs=3, align_bytes=64)
@@ -179,15 +188,14 @@ def tile_patch_reconstruction_residual_s3_kernel(
             )
             full_k4[c, g] = k4
 
-        def normalise(i, on_pool):
-            c, ii = divmod(i, CHUNK_TILES)
-            rows = flow.tile([P, PIX], F32, name="rows", bufs=8)
-            if on_pool:
+        def normalise(i):
+            rows = flow.tile([P, PIX], F32, name="rows", bufs=7)
+            if i in POOL_TILES:
                 for n in range(PIX_BANKS):
                     cols = slice(BANK * n, BANK * (n + 1))
                     nc.gpsimd.tensor_scalar(
                         out=rows[:, cols],
-                        in0=pix[c][:, ii, cols],
+                        in0=pix[i][:, cols],
                         scalar1=rstd_f32[:, i : i + 1],
                         scalar2=shift[:, i : i + 1],
                         op0=ALU.mult,
@@ -195,7 +203,7 @@ def tile_patch_reconstruction_residual_s3_kernel(
                     )
             else:
                 nc.scalar.activation(
-                    out=rows[:], in_=pix[c][:, ii, :], func=ACT.Identity, bias=shift[:, i : i + 1], scale=rstd_f32[:, i : i + 1]
+                    out=rows[:], in_=pix[i], func=ACT.Identity, bias=shift[:, i : i + 1], scale=rstd_f32[:, i : i + 1]
                 )
             target[i] = rows
 
@@ -216,110 +224,148 @@ def tile_patch_reconstruction_residual_s3_kernel(
                     stop=(g == GROUPS - 1),
                 )
             nc.vector.tensor_tensor(out=target[i][:, cols], in0=bank[:], in1=target[i][:, cols], op=ALU.subtract)
-            if i == TILES - 1:
+            if i >= 9:
                 nc.sync.dma_start(out=out_v[:, i, cols], in_=target[i][:, cols])
             elif n == PIX_BANKS - 1:
                 nc.sync.dma_start(out=out_v[:, i, :], in_=target[i][:])
 
         nc.vector.memset(pos_s_raw[:].bitcast(I32), 0)
         nc.vector.memset(head_s[:].rearrange("p g n -> p (g n)").bitcast(I32), 0)
+        make_identity(nc, ident_bf[:])
         make_identity(nc, ident[:])
-        nc.scalar.activation(out=ident_bf[:], in_=ident[:], func=ACT.Identity)
 
+        nc.sync.dma_start(out=rstd_col[:], in_=rstd.rearrange("(p i) -> p i", i=TILES))
+        nc.sync.dma_start(out=mask_col[:], in_=masked.rearrange("(p i) -> p i", i=TILES))
+        load_x("s", 0)
+        load_latents(0)
+        load_x("f", 0)
         nc.sync.dma_start(out=pos_w_raw[:].bitcast(I32), in_=pos_words[0].bitcast(I32))
         for q in range(4):
             nc.sync.dma_start(
                 out=pos_s_raw[32 * q : 32 * q + 4, :].bitcast(I32), in_=pos_scales[0, 4 * q : 4 * q + 4, :].bitcast(I32)
             )
-        load_x("f", 0)
-        load_x("s", 0)
-        load_latents(0)
-        nc.sync.dma_start(out=mask_col[:], in_=masked.rearrange("(p i) -> p i", i=TILES))
-        nc.sync.dma_start(out=embed_col[:], in_=embed.rearrange("(g p t) -> p g t", g=GROUPS, t=PACK))
         load_latents(1)
-        nc.sync.dma_start(out=mean_col[:], in_=mean.rearrange("(p i) -> p i", i=TILES))
-        nc.sync.dma_start(out=rstd_col[:], in_=rstd.rearrange("(p i) -> p i", i=TILES))
+        nc.sync.dma_start(out=embed_col[:], in_=embed.rearrange("(g p t) -> p g t", g=GROUPS, t=PACK))
         load_x("s", 1)
         load_x("f", 1)
+        nc.sync.dma_start(out=mean_col[:], in_=mean.rearrange("(p i) -> p i", i=TILES))
         for q in range(4):
             nc.sync.dma_start(
                 out=head_s[32 * q : 32 * q + 4, :, :].bitcast(I32),
                 in_=head_scales[:, 4 * q : 4 * q + 4, :].rearrange("g r n -> r g n").bitcast(I32),
             )
-        nc.sync.dma_start(out=head_w[:].bitcast(I32), in_=head_words.rearrange("g p n -> p g n").bitcast(I32))
-        load_pixels(0)
+        load_pixels(0, 2)
         load_x("s", 2)
+        nc.sync.dma_start(out=head_w[:].bitcast(I32), in_=head_words.rearrange("g p n -> p g n").bitcast(I32))
+        load_pixels(2, 2)
         load_x("f", 2)
-        load_pixels(1)
         load_x("s", 3)
+        load_pixels(4, 3)
         load_x("f", 3)
+        load_pixels(8, 3)
 
-        sort_pos(0)
-        sort_pos(1)
-        turn_x("f", 0)
+        nc.scalar.activation(out=rstd_f32[:], in_=rstd_col[:], func=ACT.Identity)
+        spread_mask(0)
         turn_x("s", 0)
-        quantize_x("f", 0)
-        for t in range(PACK):
-            open_full(0, 0, t)
-        for h in range(2):
-            bank = psum.tile([P, TILES // 2, P], BF16, name="turn", bufs=2)
-            for i in range(TILES // 2):
-                col = TILES // 2 * h + i
-                nc.tensor.transpose(bank[:, i, :], mask_col[:, col : col + 1].to_broadcast([P, P]), ident_bf[:])
-            nc.scalar.copy(out=mask_row[:, T // 2 * h : T // 2 * (h + 1)], in_=bank[:].rearrange("p i m -> p (i m)"))
+        empty_x("s", 0)
+        turn_x("f", 0)
+        empty_x("f", 0)
         sort_latents(0, nc.vector.tensor_copy)
         quantize_x("s", 0)
         quantize_latents(0)
+        sort_pos(0)
+        quantize_x("f", 0)
         sort_latents(1, nc.scalar.copy)
-        nc.vector.tensor_copy(out=rstd_f32[:], in_=rstd_col[:])
-        nc.vector.scalar_tensor_tensor(
-            out=shift[:], in0=mean_col[:], scalar=-1.0, in1=rstd_col[:], op0=ALU.mult, op1=ALU.mult
-        )
         for t in range(PACK):
-            close_full(0, 0, t)
+            full_pass("s", 0, 0, t, True)
+        for t in range(PACK):
+            full_pass("f", 0, 0, t, False)
+            empty_full(0, 0, t)
+            if t == 0:
+                sort_pos(1)
             if t == 1:
                 quantize_latents(1)
         turn_x("s", 1)
-        full_bank(0, 4)
-        full_bank(0, 5)
+        empty_x("s", 1)
         turn_x("f", 1)
-        quantize_x("s", 1)
+        empty_x("f", 1)
         weave_full(0, 0)
-        full_bank(0, 6)
+        quantize_x("s", 1)
+        full_bank(0, 4)
         quantize_x("f", 1)
+        nc.vector.scalar_tensor_tensor(
+            out=shift[:], in0=mean_col[:], scalar=-1.0, in1=rstd_col[:], op0=ALU.mult, op1=ALU.mult
+        )
+        full_bank(0, 5)
+        full_bank(0, 6)
         full_bank(0, 7)
         weave_full(0, 1)
-        for i in range(CHUNK_TILES):
-            normalise(i, True)
+        normalise(0)
+        normalise(1)
+        normalise(2)
 
-        for c in range(1, CHUNKS + 1):
-            more = c + 1 < CHUNKS
-            if c < CHUNKS:
-                quantize_at = (3, 6) if c == 1 else ((0, 2) if more else (-1, -1))
-                for b in range(GROUPS * PACK):
-                    full_bank(c, b)
-                    if b == 1 and more:
-                        turn_x("s", c + 1)
-                    if b == PACK - 1:
-                        weave_full(c, 0)
-                    if b in quantize_at:
-                        quantize_full(c - 1, quantize_at.index(b))
-                    if c == CHUNKS - 1 and b in (0, 2):
-                        quantize_full(c - 1, b // 2)
-                if more:
-                    turn_x("f", c + 1)
-                weave_full(c, 1)
-                for ii in range(CHUNK_TILES):
-                    normalise(CHUNK_TILES * c + ii, ii < 2)
-            for b in range(CHUNK_TILES * PIX_BANKS):
-                pred_bank(c - 1, b)
-                if more and b == 2:
-                    quantize_x("s", c + 1)
-                if more and b == 5:
-                    quantize_x("f", c + 1)
-                if c == CHUNKS - 1 and b == 2:
-                    quantize_full(c, 0)
-                if c == CHUNKS - 1 and b == 6:
-                    quantize_full(c, 1)
-                if more and b == 5:
-                    load_pixels(c + 1)
+        for b in range(8):
+            full_bank(1, b)
+            if b == 2:
+                quantize_full(0, 0)
+            if b == 3:
+                weave_full(1, 0)
+            if b == 5:
+                turn_x("s", 2)
+                spread_mask(1)
+                empty_x("s", 2)
+                quantize_full(0, 1)
+        weave_full(1, 1)
+        for b in range(12):
+            if b == 9:
+                normalise(4)
+            pred_bank(0, b)
+            if b == 3:
+                turn_x("f", 2)
+                empty_x("f", 2)
+                normalise(3)
+                quantize_x("s", 2)
+                quantize_full(1, 0)
+            if b == 5:
+                load_pixels(7, 1)
+            if b == 8:
+                turn_x("s", 3)
+                empty_x("s", 3)
+                quantize_x("f", 2)
+                quantize_full(1, 1)
+            if b == 11:
+                load_pixels(12, 3)
+
+        for c in range(1, CHUNKS - 1):
+            nxt, far = c + 1, c + 2
+            first = CHUNK_TILES * c
+            normalise(first + 1)
+            normalise(first + 3)
+            for kind, b in ORDER:
+                if kind == "pred":
+                    pred_bank(c, b)
+                    if b == 5:
+                        load_pixels(first + 7, 1)
+                    if b == 5 and far < CHUNKS:
+                        quantize_x("f", far)
+                    if b == (7 if far < CHUNKS else 8):
+                        quantize_full(nxt, 1)
+                        normalise(first + 4)
+                else:
+                    full_bank(nxt, b)
+                    if b == 3:
+                        weave_full(nxt, 0)
+                        normalise(first + 2)
+                    if b == 6:
+                        if far < CHUNKS:
+                            turn_x("f", far)
+                            empty_x("f", far)
+                            quantize_x("s", far)
+                        quantize_full(nxt, 0)
+                    if b == 7:
+                        weave_full(nxt, 1)
+        normalise(13)
+        normalise(14)
+        normalise(15)
+        for b in range(12):
+            pred_bank(CHUNKS - 1, b)

@@ -19,15 +19,28 @@ ACT = mybir.ActivationFunctionType
 P = 128
 PACK = 4
 BANK = 512
+QUADRANTS = 4
 TILES = T // P
 CHUNK_TILES = BANK // P
-CHUNKS = TILES // CHUNK_TILES
 GROUPS = D // (P * PACK)
+FULL_BANKS = GROUPS * PACK
 PIX_BANKS = PIX // BANK
-POOL_TILES = (0, 1, 2, 7, 11, 15)
-ORDER = [("full", b) for b in range(4)]
-ORDER = ORDER + [step for b in range(4) for step in (("pred", b), ("full", 4 + b))] + [("pred", b) for b in range(4, 12)]
-ORDER_FIRST = [("full", b) for b in range(8)] + [("pred", b) for b in range(12)]
+PRED_BANKS = CHUNK_TILES * PIX_BANKS
+
+TURN_BUFS = 2
+MX_BUFS = 6
+ROW_BUFS = 7
+FIRST_TILE_STORED_BY_BANK = 9
+BANKS_OFF_VECTOR = (9, 11)
+CHUNKS_OFF_VECTOR = 2
+
+
+def woven_order(lead):
+    rest = FULL_BANKS - lead
+    steps = [("full", b) for b in range(lead)]
+    for b in range(rest):
+        steps = steps + [("pred", b), ("full", lead + b)]
+    return steps + [("pred", b) for b in range(rest, PRED_BANKS)]
 
 
 def tile_patch_reconstruction_residual_s3_kernel(
@@ -41,20 +54,20 @@ def tile_patch_reconstruction_residual_s3_kernel(
         psum = ctx.enter_context(tc.psum_pool(name="psum", bufs=1))
         ctx.enter_context(tc.manual_schedule())
 
-        by_tile = {
+        x_by_tile = {
             "s": scatter.rearrange("(p i) k -> p i k", i=TILES),
             "f": feats.rearrange("(p i) k -> p i k", i=TILES),
         }
-        pixels_v = pixels.rearrange("(p i) n -> p i n", i=TILES)
-        out_v = out.rearrange("(p i) n -> p i n", i=TILES)
-        latents_v = latents.rearrange("(p j) d -> p j d", j=PACK)
+        pixels_by_tile = pixels.rearrange("(p i) n -> p i n", i=TILES)
+        out_by_tile = out.rearrange("(p i) n -> p i n", i=TILES)
+        latents_by_k = latents.rearrange("(p j) d -> p j d", j=PACK)
 
         ident = keep.tile([P, P], F32, name="ident")
         ident_bf = keep.tile([P, P], BF16, name="ident_bf")
         pos_w_raw = keep.tile([P, 2 * D], U8, name="pos_w_raw", align_bytes=64)
         pos_s_raw = keep.tile([P, D], U8, name="pos_s_raw", align_bytes=64)
-        pos_w = [keep.tile([P, D], U8, name="pos_w%d" % g, align_bytes=64) for g in range(GROUPS)]
-        pos_s = [keep.tile([P, D // 2], U8, name="pos_s%d" % g, align_bytes=64) for g in range(GROUPS)]
+        pos_w = [keep.tile([P, 2 * BANK], U8, name="pos_w%d" % g, align_bytes=64) for g in range(GROUPS)]
+        pos_s = [keep.tile([P, BANK], U8, name="pos_s%d" % g, align_bytes=64) for g in range(GROUPS)]
         head_w = keep.tile([P, GROUPS, 2 * PIX], U8, name="head_w", align_bytes=64)
         head_s = keep.tile([P, GROUPS, PIX], U8, name="head_s", align_bytes=64)
         lat_raw = [keep.tile([P, PACK, BANK], BF16, name="lat_raw%d" % g) for g in range(GROUPS)]
@@ -69,66 +82,66 @@ def tile_patch_reconstruction_residual_s3_kernel(
         embed_col = keep.tile([P, GROUPS, PACK], BF16, name="embed_col")
         mask_row = keep.tile([P, T], BF16, name="mask_row")
 
-        x_raw, turned, x_k4, x_q = {}, {}, {}, {}
-        pix, target = {}, {}
-        planes, full_k4, full_q, acc1 = {}, {}, {}, {}
+        x_raw, x_turned, x_k4, x_q = {}, {}, {}, {}
+        full_acc, full_planes, full_k4, full_q = {}, {}, {}, {}
+        pix, rows = {}, {}
 
         def load_x(name, c):
             raw = keep.tile([P, CHUNK_TILES, V], BF16, name="raw_%s%d" % (name, c))
-            nc.sync.dma_start(out=raw[:], in_=by_tile[name][:, CHUNK_TILES * c : CHUNK_TILES * (c + 1), :])
+            nc.sync.dma_start(out=raw[:], in_=x_by_tile[name][:, CHUNK_TILES * c : CHUNK_TILES * (c + 1), :])
             x_raw[name, c] = raw
 
-        def load_pixels(i, count):
-            part = keep.tile([P, count, PIX], BF16, name="pix%d" % i)
-            nc.sync.dma_start(out=part[:], in_=pixels_v[:, i : i + count, :])
+        def load_pixels(first, count):
+            part = keep.tile([P, count, PIX], BF16, name="pix%d" % first)
+            nc.sync.dma_start(out=part[:], in_=pixels_by_tile[:, first : first + count, :])
             for k in range(count):
-                pix[i + k] = part[:, k, :]
-
-        def spread_mask(h):
-            bank = psum.tile([P, TILES // 2, P], BF16, name="mx", bufs=6)
-            for ii in range(TILES // 2):
-                i = TILES // 2 * h + ii
-                nc.tensor.transpose(bank[:, ii, :], mask_col[:, i : i + 1].to_broadcast([P, P]), ident_bf[:])
-            nc.scalar.copy(out=mask_row[:, T // 2 * h : T // 2 * (h + 1)], in_=bank[:].rearrange("p i m -> p (i m)"))
+                pix[first + k] = part[:, k, :]
 
         def load_latents(g):
-            nc.sync.dma_start(out=lat_raw[g][:], in_=latents_v[:, :, BANK * g : BANK * (g + 1)])
+            nc.sync.dma_start(out=lat_raw[g][:], in_=latents_by_k[:, :, BANK * g : BANK * (g + 1)])
+
+        def spread_mask(half):
+            bank = psum.tile([P, TILES // 2, P], BF16, name="mx", bufs=MX_BUFS)
+            for k in range(TILES // 2):
+                i = TILES // 2 * half + k
+                nc.tensor.transpose(bank[:, k, :], mask_col[:, i : i + 1].to_broadcast([P, P]), ident_bf[:])
+            nc.scalar.copy(out=mask_row[:, T // 2 * half : T // 2 * (half + 1)], in_=bank[:].rearrange("p i m -> p (i m)"))
 
         def turn_x(name, c):
-            words = x_raw[name, c][:].rearrange("p i k -> p (i k)").bitcast(F32)
+            pairs = x_raw[name, c][:].rearrange("p i k -> p (i k)").bitcast(F32)
             banks = []
-            for h in range(2):
-                bank = psum.tile([P, 2, 2, P], F32, name="turn", bufs=2)
-                for i in range(2):
-                    w0 = (V // 2) * (2 * h + i)
+            for half in range(2):
+                bank = psum.tile([P, 2, 2, P], F32, name="turn", bufs=TURN_BUFS)
+                for k in range(2):
+                    first = (V // 2) * (2 * half + k)
                     for u in range(2):
-                        nc.tensor.transpose(bank[:, i, u, :], words[:, w0 + u : w0 + V // 2 : 2], ident[:])
+                        nc.tensor.transpose(bank[:, k, u, :], pairs[:, first + u : first + V // 2 : 2], ident[:])
                 banks.append(bank)
-            turned[name, c] = banks
+            x_turned[name, c] = banks
 
         def empty_x(name, c):
             k4 = flow.tile([P, BANK * PACK], BF16, name="x_k4", bufs=3, align_bytes=64)
-            k4_words = k4[:].bitcast(F32).rearrange("p (i r u) -> p i r u", i=CHUNK_TILES, u=2)
-            for h, bank in enumerate(turned[name, c]):
-                nc.scalar.copy(out=k4_words[:, 2 * h : 2 * h + 2, :, :], in_=bank[:].rearrange("p i u r -> p i r u"))
+            k4_pairs = k4[:].bitcast(F32).rearrange("p (i m u) -> p i m u", i=CHUNK_TILES, u=2)
+            for half, bank in enumerate(x_turned[name, c]):
+                nc.scalar.copy(out=k4_pairs[:, 2 * half : 2 * half + 2, :, :], in_=bank[:].rearrange("p i u m -> p i m u"))
             x_k4[name, c] = k4
 
-        def quantize(src, tag, bufs):
-            codes = flow.tile([P, BANK], U32, name=tag + "_c", bufs=bufs, align_bytes=64)
-            scales = flow.tile([P, BANK], U8, name=tag + "_s", bufs=bufs, align_bytes=64)
-            nc.vector.quantize_mx(out=codes[:].bitcast(FP8X4), scales=scales[:], in_=src[:])
+        def quantize(k4, tag):
+            codes = flow.tile([P, BANK], U32, name=tag + "_c", bufs=4, align_bytes=64)
+            scales = flow.tile([P, BANK], U8, name=tag + "_s", bufs=4, align_bytes=64)
+            nc.vector.quantize_mx(out=codes[:].bitcast(FP8X4), scales=scales[:], in_=k4[:])
             return codes, scales
 
         def quantize_x(name, c):
-            x_q[name, c] = quantize(x_k4[name, c], "xq", 4)
+            x_q[name, c] = quantize(x_k4[name, c], "xq")
 
         def quantize_full(c, g):
-            full_q[c, g] = quantize(full_k4[c, g], "fq", 4)
+            full_q[c, g] = quantize(full_k4[c, g], "fq")
 
         def sort_pos(g):
             nc.vector.tensor_copy(
                 out=pos_w[g][:].rearrange("p (t m b) -> p t m b", t=PACK, b=2),
-                in_=pos_w_raw[:, D * g : D * (g + 1)].rearrange("p (m t b) -> p t m b", t=PACK, b=2),
+                in_=pos_w_raw[:, 2 * BANK * g : 2 * BANK * (g + 1)].rearrange("p (m t b) -> p t m b", t=PACK, b=2),
             )
             nc.vector.tensor_copy(
                 out=pos_s[g][:].rearrange("p (t m) -> p t m", t=PACK),
@@ -144,90 +157,95 @@ def tile_patch_reconstruction_residual_s3_kernel(
         def quantize_latents(g):
             nc.vector.quantize_mx(out=lat_c[g][:].bitcast(FP8X4), scales=lat_s[g][:], in_=lat_k4[g][:])
 
-        def full_pass(name, c, g, t, start):
-            if start:
-                acc1[c, g, t] = psum.tile([P, BANK], F32, name="mx", bufs=6)
-            codes, scales = x_q[name, c]
-            if name == "s":
+        def full_pass(name, c, g, t):
+            opens = name == "s"
+            if opens:
+                full_acc[c, g, t] = psum.tile([P, BANK], F32, name="mx", bufs=MX_BUFS)
                 weights, weight_scales = lat_c[g][:, P * t : P * (t + 1)].bitcast(FP8X4), lat_s[g]
             else:
                 weights, weight_scales = pos_w[g][:, 2 * P * t : 2 * P * (t + 1)].bitcast(FP4X4), pos_s[g]
+            codes, scales = x_q[name, c]
             nc.tensor.matmul_mx(
-                out=acc1[c, g, t][:],
+                out=full_acc[c, g, t][:],
                 lhsT=weights,
                 lhsT_scale=weight_scales[:, P * t : P * (t + 1)],
                 rhs=codes[:].bitcast(FP8X4),
                 rhs_scale=scales[:],
-                start=start,
-                stop=not start,
+                start=opens,
+                stop=not opens,
             )
 
         def empty_full(c, g, t):
             if t == 0:
-                planes[c, g] = flow.tile([P, PACK, BANK], BF16, name="planes", bufs=3)
+                full_planes[c, g] = flow.tile([P, PACK, BANK], BF16, name="planes", bufs=3)
             nc.vector.scalar_tensor_tensor(
-                out=planes[c, g][:, t, :],
+                out=full_planes[c, g][:, t, :],
                 in0=mask_row[:, BANK * c : BANK * (c + 1)],
                 scalar=embed_col[:, g, t : t + 1],
-                in1=acc1[c, g, t][:],
+                in1=full_acc[c, g, t][:],
                 op0=ALU.mult,
                 op1=ALU.add,
             )
 
         def full_bank(c, b):
             g, t = divmod(b, PACK)
-            full_pass("s", c, g, t, True)
-            full_pass("f", c, g, t, False)
+            full_pass("s", c, g, t)
+            full_pass("f", c, g, t)
             empty_full(c, g, t)
 
-        def weave_full(c, g):
+        def interleave_full(c, g):
             k4 = flow.tile([P, BANK * PACK], BF16, name="full_k4", bufs=3, align_bytes=64)
             nc.scalar.copy(
-                out=k4[:].rearrange("p (q i t) -> p q t i", i=4, t=PACK),
-                in_=planes[c, g][:].rearrange("p t (q i) -> p q t i", i=4),
+                out=k4[:].rearrange("p (q n t) -> p q t n", n=4, t=PACK),
+                in_=full_planes[c, g][:].rearrange("p t (q n) -> p q t n", n=4),
             )
             full_k4[c, g] = k4
 
-        def normalise(i):
-            rows = flow.tile([P, PIX], F32, name="rows", bufs=7)
-            if i in POOL_TILES:
-                for n in range(PIX_BANKS):
-                    cols = slice(BANK * n, BANK * (n + 1))
-                    nc.gpsimd.tensor_scalar(
-                        out=rows[:, cols],
-                        in0=pix[i][:, cols],
-                        scalar1=rstd_f32[:, i : i + 1],
-                        scalar2=shift[:, i : i + 1],
-                        op0=ALU.mult,
-                        op1=ALU.add,
-                    )
-            else:
-                nc.scalar.activation(
-                    out=rows[:], in_=pix[i], func=ACT.Identity, bias=shift[:, i : i + 1], scale=rstd_f32[:, i : i + 1]
+        def normalise_on_scalar(i):
+            rows[i] = flow.tile([P, PIX], F32, name="rows", bufs=ROW_BUFS)
+            nc.scalar.activation(
+                out=rows[i][:], in_=pix[i], func=ACT.Identity, bias=shift[:, i : i + 1], scale=rstd_f32[:, i : i + 1]
+            )
+
+        def normalise_on_gpsimd(i):
+            rows[i] = flow.tile([P, PIX], F32, name="rows", bufs=ROW_BUFS)
+            for n in range(PIX_BANKS):
+                cols = slice(BANK * n, BANK * (n + 1))
+                nc.gpsimd.tensor_scalar(
+                    out=rows[i][:, cols],
+                    in0=pix[i][:, cols],
+                    scalar1=rstd_f32[:, i : i + 1],
+                    scalar2=shift[:, i : i + 1],
+                    op0=ALU.mult,
+                    op1=ALU.add,
                 )
-            target[i] = rows
 
         def pred_bank(c, b):
-            ii, n = divmod(b, PIX_BANKS)
-            i = CHUNK_TILES * c + ii
+            k, n = divmod(b, PIX_BANKS)
+            i = CHUNK_TILES * c + k
             cols = slice(BANK * n, BANK * (n + 1))
-            bank = psum.tile([P, BANK], F32, name="mx", bufs=6)
+            bank = psum.tile([P, BANK], F32, name="mx", bufs=MX_BUFS)
             for g in range(GROUPS):
                 codes, scales = full_q[c, g]
                 nc.tensor.matmul_mx(
                     out=bank[:],
-                    lhsT=codes[:, P * ii : P * (ii + 1)].bitcast(FP8X4),
-                    lhsT_scale=scales[:, P * ii : P * (ii + 1)],
+                    lhsT=codes[:, P * k : P * (k + 1)].bitcast(FP8X4),
+                    lhsT_scale=scales[:, P * k : P * (k + 1)],
                     rhs=head_w[:, g, 2 * BANK * n : 2 * BANK * (n + 1)].bitcast(FP4X4),
                     rhs_scale=head_s[:, g, cols],
                     start=(g == 0),
                     stop=(g == GROUPS - 1),
                 )
-            nc.vector.tensor_tensor(out=target[i][:, cols], in0=bank[:], in1=target[i][:, cols], op=ALU.subtract)
-            if i >= 9:
-                nc.sync.dma_start(out=out_v[:, i, cols], in_=target[i][:, cols])
+            if c < CHUNKS_OFF_VECTOR and b in BANKS_OFF_VECTOR:
+                pred = flow.tile([P, BANK], F32, name="pred", bufs=3)
+                nc.scalar.copy(out=pred[:], in_=bank[:])
+                nc.gpsimd.tensor_tensor(out=rows[i][:, cols], in0=pred[:], in1=rows[i][:, cols], op=ALU.subtract)
+            else:
+                nc.vector.tensor_tensor(out=rows[i][:, cols], in0=bank[:], in1=rows[i][:, cols], op=ALU.subtract)
+            if i >= FIRST_TILE_STORED_BY_BANK:
+                nc.sync.dma_start(out=out_by_tile[:, i, cols], in_=rows[i][:, cols])
             elif n == PIX_BANKS - 1:
-                nc.sync.dma_start(out=out_v[:, i, :], in_=target[i][:])
+                nc.sync.dma_start(out=out_by_tile[:, i, :], in_=rows[i][:])
 
         nc.vector.memset(pos_s_raw[:].bitcast(I32), 0)
         nc.vector.memset(head_s[:].rearrange("p g n -> p (g n)").bitcast(I32), 0)
@@ -240,7 +258,7 @@ def tile_patch_reconstruction_residual_s3_kernel(
         load_latents(0)
         load_x("f", 0)
         nc.sync.dma_start(out=pos_w_raw[:].bitcast(I32), in_=pos_words[0].bitcast(I32))
-        for q in range(4):
+        for q in range(QUADRANTS):
             nc.sync.dma_start(
                 out=pos_s_raw[32 * q : 32 * q + 4, :].bitcast(I32), in_=pos_scales[0, 4 * q : 4 * q + 4, :].bitcast(I32)
             )
@@ -249,7 +267,7 @@ def tile_patch_reconstruction_residual_s3_kernel(
         load_x("s", 1)
         load_x("f", 1)
         nc.sync.dma_start(out=mean_col[:], in_=mean.rearrange("(p i) -> p i", i=TILES))
-        for q in range(4):
+        for q in range(QUADRANTS):
             nc.sync.dma_start(
                 out=head_s[32 * q : 32 * q + 4, :, :].bitcast(I32),
                 in_=head_scales[:, 4 * q : 4 * q + 4, :].rearrange("g r n -> r g n").bitcast(I32),
@@ -277,9 +295,9 @@ def tile_patch_reconstruction_residual_s3_kernel(
         quantize_x("f", 0)
         sort_latents(1, nc.scalar.copy)
         for t in range(PACK):
-            full_pass("s", 0, 0, t, True)
+            full_pass("s", 0, 0, t)
         for t in range(PACK):
-            full_pass("f", 0, 0, t, False)
+            full_pass("f", 0, 0, t)
             empty_full(0, 0, t)
             if t == 0:
                 sort_pos(1)
@@ -289,41 +307,39 @@ def tile_patch_reconstruction_residual_s3_kernel(
         empty_x("s", 1)
         turn_x("f", 1)
         empty_x("f", 1)
-        weave_full(0, 0)
-        quantize_x("s", 1)
-        full_bank(0, 4)
-        quantize_x("f", 1)
+        interleave_full(0, 0)
         nc.vector.scalar_tensor_tensor(
             out=shift[:], in0=mean_col[:], scalar=-1.0, in1=rstd_col[:], op0=ALU.mult, op1=ALU.mult
         )
-        full_bank(0, 5)
-        full_bank(0, 6)
-        full_bank(0, 7)
-        weave_full(0, 1)
-        normalise(0)
-        normalise(1)
-        normalise(2)
+        normalise_on_gpsimd(0)
+        quantize_x("s", 1)
+        full_bank(0, 4)
+        quantize_x("f", 1)
+        for b in range(5, FULL_BANKS):
+            full_bank(0, b)
+        interleave_full(0, 1)
+        normalise_on_gpsimd(1)
+        normalise_on_gpsimd(2)
 
-        for b in range(8):
+        for b in range(FULL_BANKS):
             full_bank(1, b)
-            if b == 2:
-                quantize_full(0, 0)
-            if b == 3:
-                weave_full(1, 0)
-            if b == 5:
+            if b == PACK - 1:
+                interleave_full(1, 0)
+            if b == PACK + 1:
                 turn_x("s", 2)
                 spread_mask(1)
                 empty_x("s", 2)
+                quantize_full(0, 0)
                 quantize_full(0, 1)
-        weave_full(1, 1)
-        for b in range(12):
-            if b == 9:
-                normalise(4)
+        interleave_full(1, 1)
+
+        normalise_on_gpsimd(4)
+        for b in range(PRED_BANKS):
             pred_bank(0, b)
             if b == 3:
                 turn_x("f", 2)
                 empty_x("f", 2)
-                normalise(3)
+                normalise_on_scalar(3)
                 quantize_x("s", 2)
                 quantize_full(1, 0)
             if b == 5:
@@ -333,39 +349,51 @@ def tile_patch_reconstruction_residual_s3_kernel(
                 empty_x("s", 3)
                 quantize_x("f", 2)
                 quantize_full(1, 1)
-            if b == 11:
-                load_pixels(12, 3)
+        load_pixels(12, CHUNK_TILES)
 
-        for c in range(1, CHUNKS - 1):
-            nxt, far = c + 1, c + 2
-            first = CHUNK_TILES * c
-            normalise(first + 1)
-            normalise(first + 3)
-            for kind, b in ORDER:
-                if kind == "pred":
-                    pred_bank(c, b)
-                    if b == 5:
-                        load_pixels(first + 7, 1)
-                    if b == 5 and far < CHUNKS:
-                        quantize_x("f", far)
-                    if b == (7 if far < CHUNKS else 8):
-                        quantize_full(nxt, 1)
-                        normalise(first + 4)
-                else:
-                    full_bank(nxt, b)
-                    if b == 3:
-                        weave_full(nxt, 0)
-                        normalise(first + 2)
-                    if b == 6:
-                        if far < CHUNKS:
-                            turn_x("f", far)
-                            empty_x("f", far)
-                            quantize_x("s", far)
-                        quantize_full(nxt, 0)
-                    if b == 7:
-                        weave_full(nxt, 1)
-        normalise(13)
-        normalise(14)
-        normalise(15)
-        for b in range(12):
-            pred_bank(CHUNKS - 1, b)
+        normalise_on_scalar(5)
+        normalise_on_gpsimd(7)
+        for kind, b in woven_order(PACK):
+            if kind == "full":
+                full_bank(2, b)
+                if b == PACK - 1:
+                    interleave_full(2, 0)
+                    normalise_on_scalar(6)
+                if b == FULL_BANKS - 2:
+                    turn_x("f", 3)
+                    empty_x("f", 3)
+                    quantize_x("s", 3)
+                    quantize_full(2, 0)
+                if b == FULL_BANKS - 1:
+                    interleave_full(2, 1)
+            else:
+                pred_bank(1, b)
+                if b == 5:
+                    load_pixels(11, 1)
+                if b == 7:
+                    quantize_x("f", 3)
+                if b == 8:
+                    quantize_full(2, 1)
+        normalise_on_scalar(8)
+
+        normalise_on_scalar(9)
+        normalise_on_gpsimd(11)
+        for kind, b in woven_order(PACK + 1):
+            if kind == "full":
+                full_bank(3, b)
+                if b == PACK - 1:
+                    interleave_full(3, 0)
+                    normalise_on_gpsimd(10)
+                if b == FULL_BANKS - 1:
+                    interleave_full(3, 1)
+            else:
+                pred_bank(2, b)
+                if b == 4:
+                    quantize_full(3, 0)
+                if b == 8:
+                    quantize_full(3, 1)
+
+        for i in range(TILES - CHUNK_TILES, TILES):
+            normalise_on_scalar(i)
+        for b in range(PRED_BANKS):
+            pred_bank(3, b)

from contextlib import ExitStack

import concourse.mybir as mybir
from concourse.masks import make_identity

T, V, C, D, PIX = 2048, 512, 512, 1024, 1536
FLOPS = 2 * T * (V * D + C * D + D * PIX)

F32 = mybir.dt.float32
BF16 = mybir.dt.bfloat16
I32 = mybir.dt.int32
U32 = mybir.dt.uint32
U8 = mybir.dt.uint8
FP8X4 = mybir.dt.float8_e4m3fn_x4
FP4X4 = mybir.dt.float4_e2m1fn_x4
ALU = mybir.AluOpType
ACT = mybir.ActivationFunctionType

P = 128
PACK = 4
BANK = 512
QUADRANTS = 4
TILES = T // P
CHUNK_TILES = BANK // P
GROUPS = D // (P * PACK)
FULL_BANKS = GROUPS * PACK
PIX_BANKS = PIX // BANK
PRED_BANKS = CHUNK_TILES * PIX_BANKS

TURN_BUFS = 2
MX_BUFS = 6
ROW_BUFS = 7
FIRST_TILE_STORED_BY_BANK = 9
BANKS_OFF_VECTOR = (9, 11)
CHUNKS_OFF_VECTOR = 2


def woven_order(lead):
    rest = FULL_BANKS - lead
    steps = [("full", b) for b in range(lead)]
    for b in range(rest):
        steps = steps + [("pred", b), ("full", lead + b)]
    return steps + [("pred", b) for b in range(rest, PRED_BANKS)]


def tile_patch_reconstruction_residual_s3_kernel(
    tc, scatter, latents, feats, pos_words, pos_scales, masked, embed, head_words, head_scales, pixels, mean, rstd, out
):
    nc = tc.nc

    with ExitStack() as ctx:
        keep = ctx.enter_context(tc.tile_pool(name="keep", bufs=1))
        flow = ctx.enter_context(tc.tile_pool(name="flow", bufs=1))
        psum = ctx.enter_context(tc.psum_pool(name="psum", bufs=1))
        ctx.enter_context(tc.manual_schedule())

        x_by_tile = {
            "s": scatter.rearrange("(p i) k -> p i k", i=TILES),
            "f": feats.rearrange("(p i) k -> p i k", i=TILES),
        }
        pixels_by_tile = pixels.rearrange("(p i) n -> p i n", i=TILES)
        out_by_tile = out.rearrange("(p i) n -> p i n", i=TILES)
        latents_by_k = latents.rearrange("(p j) d -> p j d", j=PACK)

        ident = keep.tile([P, P], F32, name="ident")
        ident_bf = keep.tile([P, P], BF16, name="ident_bf")
        pos_w_raw = keep.tile([P, 2 * D], U8, name="pos_w_raw", align_bytes=64)
        pos_s_raw = keep.tile([P, D], U8, name="pos_s_raw", align_bytes=64)
        pos_w = [keep.tile([P, 2 * BANK], U8, name="pos_w%d" % g, align_bytes=64) for g in range(GROUPS)]
        pos_s = [keep.tile([P, BANK], U8, name="pos_s%d" % g, align_bytes=64) for g in range(GROUPS)]
        head_w = keep.tile([P, GROUPS, 2 * PIX], U8, name="head_w", align_bytes=64)
        head_s = keep.tile([P, GROUPS, PIX], U8, name="head_s", align_bytes=64)
        lat_raw = [keep.tile([P, PACK, BANK], BF16, name="lat_raw%d" % g) for g in range(GROUPS)]
        lat_k4 = [keep.tile([P, BANK * PACK], BF16, name="lat_k4%d" % g, align_bytes=64) for g in range(GROUPS)]
        lat_c = [keep.tile([P, BANK], U32, name="lat_c%d" % g, align_bytes=64) for g in range(GROUPS)]
        lat_s = [keep.tile([P, BANK], U8, name="lat_s%d" % g, align_bytes=64) for g in range(GROUPS)]
        mask_col = keep.tile([P, TILES], BF16, name="mask_col")
        mean_col = keep.tile([P, TILES], BF16, name="mean_col")
        rstd_col = keep.tile([P, TILES], BF16, name="rstd_col")
        rstd_f32 = keep.tile([P, TILES], F32, name="rstd_f32")
        shift = keep.tile([P, TILES], F32, name="shift")
        embed_col = keep.tile([P, GROUPS, PACK], BF16, name="embed_col")
        mask_row = keep.tile([P, T], BF16, name="mask_row")

        x_raw, x_turned, x_k4, x_q = {}, {}, {}, {}
        full_acc, full_planes, full_k4, full_q = {}, {}, {}, {}
        pix, rows = {}, {}

        def load_x(name, c):
            raw = keep.tile([P, CHUNK_TILES, V], BF16, name="raw_%s%d" % (name, c))
            nc.sync.dma_start(out=raw[:], in_=x_by_tile[name][:, CHUNK_TILES * c : CHUNK_TILES * (c + 1), :])
            x_raw[name, c] = raw

        def load_pixels(first, count):
            part = keep.tile([P, count, PIX], BF16, name="pix%d" % first)
            nc.sync.dma_start(out=part[:], in_=pixels_by_tile[:, first : first + count, :])
            for k in range(count):
                pix[first + k] = part[:, k, :]

        def load_latents(g):
            nc.sync.dma_start(out=lat_raw[g][:], in_=latents_by_k[:, :, BANK * g : BANK * (g + 1)])

        def spread_mask(half):
            bank = psum.tile([P, TILES // 2, P], BF16, name="mx", bufs=MX_BUFS)
            for k in range(TILES // 2):
                i = TILES // 2 * half + k
                nc.tensor.transpose(bank[:, k, :], mask_col[:, i : i + 1].to_broadcast([P, P]), ident_bf[:])
            nc.scalar.copy(out=mask_row[:, T // 2 * half : T // 2 * (half + 1)], in_=bank[:].rearrange("p i m -> p (i m)"))

        def turn_x(name, c):
            pairs = x_raw[name, c][:].rearrange("p i k -> p (i k)").bitcast(F32)
            banks = []
            for half in range(2):
                bank = psum.tile([P, 2, 2, P], F32, name="turn", bufs=TURN_BUFS)
                for k in range(2):
                    first = (V // 2) * (2 * half + k)
                    for u in range(2):
                        nc.tensor.transpose(bank[:, k, u, :], pairs[:, first + u : first + V // 2 : 2], ident[:])
                banks.append(bank)
            x_turned[name, c] = banks

        def empty_x(name, c):
            k4 = flow.tile([P, BANK * PACK], BF16, name="x_k4", bufs=3, align_bytes=64)
            k4_pairs = k4[:].bitcast(F32).rearrange("p (i m u) -> p i m u", i=CHUNK_TILES, u=2)
            for half, bank in enumerate(x_turned[name, c]):
                nc.scalar.copy(out=k4_pairs[:, 2 * half : 2 * half + 2, :, :], in_=bank[:].rearrange("p i u m -> p i m u"))
            x_k4[name, c] = k4

        def quantize(k4, tag):
            codes = flow.tile([P, BANK], U32, name=tag + "_c", bufs=4, align_bytes=64)
            scales = flow.tile([P, BANK], U8, name=tag + "_s", bufs=4, align_bytes=64)
            nc.vector.quantize_mx(out=codes[:].bitcast(FP8X4), scales=scales[:], in_=k4[:])
            return codes, scales

        def quantize_x(name, c):
            x_q[name, c] = quantize(x_k4[name, c], "xq")

        def quantize_full(c, g):
            full_q[c, g] = quantize(full_k4[c, g], "fq")

        def sort_pos(g):
            nc.vector.tensor_copy(
                out=pos_w[g][:].rearrange("p (t m b) -> p t m b", t=PACK, b=2),
                in_=pos_w_raw[:, 2 * BANK * g : 2 * BANK * (g + 1)].rearrange("p (m t b) -> p t m b", t=PACK, b=2),
            )
            nc.vector.tensor_copy(
                out=pos_s[g][:].rearrange("p (t m) -> p t m", t=PACK),
                in_=pos_s_raw[:, BANK * g : BANK * (g + 1)].rearrange("p (m t) -> p t m", t=PACK),
            )

        def sort_latents(g, copy):
            copy(
                out=lat_k4[g][:].rearrange("p (t m j) -> p t m j", t=PACK, j=PACK),
                in_=lat_raw[g][:].rearrange("p j (m t) -> p t m j", t=PACK),
            )

        def quantize_latents(g):
            nc.vector.quantize_mx(out=lat_c[g][:].bitcast(FP8X4), scales=lat_s[g][:], in_=lat_k4[g][:])

        def full_pass(name, c, g, t):
            opens = name == "s"
            if opens:
                full_acc[c, g, t] = psum.tile([P, BANK], F32, name="mx", bufs=MX_BUFS)
                weights, weight_scales = lat_c[g][:, P * t : P * (t + 1)].bitcast(FP8X4), lat_s[g]
            else:
                weights, weight_scales = pos_w[g][:, 2 * P * t : 2 * P * (t + 1)].bitcast(FP4X4), pos_s[g]
            codes, scales = x_q[name, c]
            nc.tensor.matmul_mx(
                out=full_acc[c, g, t][:],
                lhsT=weights,
                lhsT_scale=weight_scales[:, P * t : P * (t + 1)],
                rhs=codes[:].bitcast(FP8X4),
                rhs_scale=scales[:],
                start=opens,
                stop=not opens,
            )

        def empty_full(c, g, t):
            if t == 0:
                full_planes[c, g] = flow.tile([P, PACK, BANK], BF16, name="planes", bufs=3)
            nc.vector.scalar_tensor_tensor(
                out=full_planes[c, g][:, t, :],
                in0=mask_row[:, BANK * c : BANK * (c + 1)],
                scalar=embed_col[:, g, t : t + 1],
                in1=full_acc[c, g, t][:],
                op0=ALU.mult,
                op1=ALU.add,
            )

        def full_bank(c, b):
            g, t = divmod(b, PACK)
            full_pass("s", c, g, t)
            full_pass("f", c, g, t)
            empty_full(c, g, t)

        def interleave_full(c, g):
            k4 = flow.tile([P, BANK * PACK], BF16, name="full_k4", bufs=3, align_bytes=64)
            nc.scalar.copy(
                out=k4[:].rearrange("p (q n t) -> p q t n", n=4, t=PACK),
                in_=full_planes[c, g][:].rearrange("p t (q n) -> p q t n", n=4),
            )
            full_k4[c, g] = k4

        def normalise_on_scalar(i):
            rows[i] = flow.tile([P, PIX], F32, name="rows", bufs=ROW_BUFS)
            nc.scalar.activation(
                out=rows[i][:], in_=pix[i], func=ACT.Identity, bias=shift[:, i : i + 1], scale=rstd_f32[:, i : i + 1]
            )

        def normalise_on_gpsimd(i):
            rows[i] = flow.tile([P, PIX], F32, name="rows", bufs=ROW_BUFS)
            for n in range(PIX_BANKS):
                cols = slice(BANK * n, BANK * (n + 1))
                nc.gpsimd.tensor_scalar(
                    out=rows[i][:, cols],
                    in0=pix[i][:, cols],
                    scalar1=rstd_f32[:, i : i + 1],
                    scalar2=shift[:, i : i + 1],
                    op0=ALU.mult,
                    op1=ALU.add,
                )

        def pred_bank(c, b):
            k, n = divmod(b, PIX_BANKS)
            i = CHUNK_TILES * c + k
            cols = slice(BANK * n, BANK * (n + 1))
            bank = psum.tile([P, BANK], F32, name="mx", bufs=MX_BUFS)
            for g in range(GROUPS):
                codes, scales = full_q[c, g]
                nc.tensor.matmul_mx(
                    out=bank[:],
                    lhsT=codes[:, P * k : P * (k + 1)].bitcast(FP8X4),
                    lhsT_scale=scales[:, P * k : P * (k + 1)],
                    rhs=head_w[:, g, 2 * BANK * n : 2 * BANK * (n + 1)].bitcast(FP4X4),
                    rhs_scale=head_s[:, g, cols],
                    start=(g == 0),
                    stop=(g == GROUPS - 1),
                )
            if c < CHUNKS_OFF_VECTOR and b in BANKS_OFF_VECTOR:
                pred = flow.tile([P, BANK], F32, name="pred", bufs=3)
                nc.scalar.copy(out=pred[:], in_=bank[:])
                nc.gpsimd.tensor_tensor(out=rows[i][:, cols], in0=pred[:], in1=rows[i][:, cols], op=ALU.subtract)
            else:
                nc.vector.tensor_tensor(out=rows[i][:, cols], in0=bank[:], in1=rows[i][:, cols], op=ALU.subtract)
            if i >= FIRST_TILE_STORED_BY_BANK:
                nc.sync.dma_start(out=out_by_tile[:, i, cols], in_=rows[i][:, cols])
            elif n == PIX_BANKS - 1:
                nc.sync.dma_start(out=out_by_tile[:, i, :], in_=rows[i][:])

        nc.vector.memset(pos_s_raw[:].bitcast(I32), 0)
        nc.vector.memset(head_s[:].rearrange("p g n -> p (g n)").bitcast(I32), 0)
        make_identity(nc, ident_bf[:])
        make_identity(nc, ident[:])

        nc.sync.dma_start(out=rstd_col[:], in_=rstd.rearrange("(p i) -> p i", i=TILES))
        nc.sync.dma_start(out=mask_col[:], in_=masked.rearrange("(p i) -> p i", i=TILES))
        load_x("s", 0)
        load_latents(0)
        load_x("f", 0)
        nc.sync.dma_start(out=pos_w_raw[:].bitcast(I32), in_=pos_words[0].bitcast(I32))
        for q in range(QUADRANTS):
            nc.sync.dma_start(
                out=pos_s_raw[32 * q : 32 * q + 4, :].bitcast(I32), in_=pos_scales[0, 4 * q : 4 * q + 4, :].bitcast(I32)
            )
        load_latents(1)
        nc.sync.dma_start(out=embed_col[:], in_=embed.rearrange("(g p t) -> p g t", g=GROUPS, t=PACK))
        load_x("s", 1)
        load_x("f", 1)
        nc.sync.dma_start(out=mean_col[:], in_=mean.rearrange("(p i) -> p i", i=TILES))
        for q in range(QUADRANTS):
            nc.sync.dma_start(
                out=head_s[32 * q : 32 * q + 4, :, :].bitcast(I32),
                in_=head_scales[:, 4 * q : 4 * q + 4, :].rearrange("g r n -> r g n").bitcast(I32),
            )
        load_pixels(0, 2)
        load_x("s", 2)
        nc.sync.dma_start(out=head_w[:].bitcast(I32), in_=head_words.rearrange("g p n -> p g n").bitcast(I32))
        load_pixels(2, 2)
        load_x("f", 2)
        load_x("s", 3)
        load_pixels(4, 3)
        load_x("f", 3)
        load_pixels(8, 3)

        nc.scalar.activation(out=rstd_f32[:], in_=rstd_col[:], func=ACT.Identity)
        spread_mask(0)
        turn_x("s", 0)
        empty_x("s", 0)
        turn_x("f", 0)
        empty_x("f", 0)
        sort_latents(0, nc.vector.tensor_copy)
        quantize_x("s", 0)
        quantize_latents(0)
        sort_pos(0)
        quantize_x("f", 0)
        sort_latents(1, nc.scalar.copy)
        for t in range(PACK):
            full_pass("s", 0, 0, t)
        for t in range(PACK):
            full_pass("f", 0, 0, t)
            empty_full(0, 0, t)
            if t == 0:
                sort_pos(1)
            if t == 1:
                quantize_latents(1)
        turn_x("s", 1)
        empty_x("s", 1)
        turn_x("f", 1)
        empty_x("f", 1)
        interleave_full(0, 0)
        nc.vector.scalar_tensor_tensor(
            out=shift[:], in0=mean_col[:], scalar=-1.0, in1=rstd_col[:], op0=ALU.mult, op1=ALU.mult
        )
        normalise_on_gpsimd(0)
        quantize_x("s", 1)
        full_bank(0, 4)
        quantize_x("f", 1)
        for b in range(5, FULL_BANKS):
            full_bank(0, b)
        interleave_full(0, 1)
        normalise_on_gpsimd(1)
        normalise_on_gpsimd(2)

        for b in range(FULL_BANKS):
            full_bank(1, b)
            if b == PACK - 1:
                interleave_full(1, 0)
            if b == PACK + 1:
                turn_x("s", 2)
                spread_mask(1)
                empty_x("s", 2)
                quantize_full(0, 0)
                quantize_full(0, 1)
        interleave_full(1, 1)

        normalise_on_gpsimd(4)
        for b in range(PRED_BANKS):
            pred_bank(0, b)
            if b == 3:
                turn_x("f", 2)
                empty_x("f", 2)
                normalise_on_scalar(3)
                quantize_x("s", 2)
                quantize_full(1, 0)
            if b == 5:
                load_pixels(7, 1)
            if b == 8:
                turn_x("s", 3)
                empty_x("s", 3)
                quantize_x("f", 2)
                quantize_full(1, 1)
        load_pixels(12, CHUNK_TILES)

        normalise_on_scalar(5)
        normalise_on_gpsimd(7)
        for kind, b in woven_order(PACK):
            if kind == "full":
                full_bank(2, b)
                if b == PACK - 1:
                    interleave_full(2, 0)
                    normalise_on_scalar(6)
                if b == FULL_BANKS - 2:
                    turn_x("f", 3)
                    empty_x("f", 3)
                    quantize_x("s", 3)
                    quantize_full(2, 0)
                if b == FULL_BANKS - 1:
                    interleave_full(2, 1)
            else:
                pred_bank(1, b)
                if b == 5:
                    load_pixels(11, 1)
                if b == 7:
                    quantize_x("f", 3)
                if b == 8:
                    quantize_full(2, 1)
        normalise_on_scalar(8)

        normalise_on_scalar(9)
        normalise_on_gpsimd(11)
        for kind, b in woven_order(PACK + 1):
            if kind == "full":
                full_bank(3, b)
                if b == PACK - 1:
                    interleave_full(3, 0)
                    normalise_on_gpsimd(10)
                if b == FULL_BANKS - 1:
                    interleave_full(3, 1)
            else:
                pred_bank(2, b)
                if b == 4:
                    quantize_full(3, 0)
                if b == 8:
                    quantize_full(3, 1)

        for i in range(TILES - CHUNK_TILES, TILES):
            normalise_on_scalar(i)
        for b in range(PRED_BANKS):
            pred_bank(3, b)
